import numpy as np
import ml_dtypes


def mxq(x, axis, fmt="e4m3"):
    dtype, down = {"e4m3": (ml_dtypes.float8_e4m3fn, 7), "e5m2": (ml_dtypes.float8_e5m2, 14)}[fmt]
    v = np.moveaxis(np.asarray(x, np.float32).astype(ml_dtypes.bfloat16).astype(np.float64), axis, -1)
    blocks = v.reshape(v.shape[:-1] + (-1, 32))
    amax = np.abs(blocks).max(-1, keepdims=True)
    byte = np.maximum(np.where(amax > 0, np.frexp(amax)[1] - 1 + 127, 0) - down, 1)
    scale = np.exp2(byte - 127.0)
    codes = (blocks / scale).astype(np.float32).astype(dtype).astype(np.float64)
    return np.moveaxis((codes * scale).reshape(v.shape), -1, axis)


WIDE = False


def mx_kscale(k):
    if not WIDE:
        return np.ones(k)
    levels = np.array([10, -10, 5, -5, 0])
    if k % 512:
        return np.exp2(np.random.permutation(np.resize(levels, k // 32))).repeat(32)
    a = np.empty((k // 512, 16))
    for p in range(k // 512):
        a[p, :8] = np.random.permutation(np.resize(levels, 8))
        for g in range(8):
            far = levels[np.abs(levels - a[p, g]) >= 10]
            a[p, g + 8] = far[np.random.randint(len(far))]
    return np.exp2(a.ravel()).repeat(32)


def f64(x):
    return np.asarray(x).astype(np.float64)


def striped(idx):
    return np.tile(np.asarray(idx).reshape(-1, 16).T, (8, 1)).astype(np.uint16)


def unstriped(offs):
    return offs[:16].T.reshape(-1).astype(np.int64)


D, T, I, Q, E, U = 512, 2048, 512, 128, 512, 1024


def setup_inputs():
    n = np.random.standard_normal
    idx = np.random.permutation(T)[:I]
    idx2 = np.random.permutation(U)[:I]
    fd = mx_kscale(D)
    fi = mx_kscale(I)
    ti = np.ones(T)
    ti[idx] = fi
    return {
        "query": (n((D, Q)) * 0.9 / np.sqrt(D) * fd[:, None]).astype(np.float32),
        "keys": (n((D, T)) / fd[:, None]).astype(np.float32),
        "notes": (n((D, U)) / fd[:, None]).astype(np.float32),
        "os": (np.random.uniform(0.02, 0.08, (1, I)) * fi).astype(np.float32),
        "vals": (n((E, T)) / ti).astype(np.float32),
        "offs": striped(idx),
        "offs2": striped(idx2),
    }


def reference(query, keys, notes, os, vals, offs, offs2):
    idx = unstriped(offs)
    idx2 = unstriped(offs2)
    zk = np.abs(f64(keys)[:, idx] - f64(notes)[:, idx2])
    queryq = mxq(f64(query), 0, "e4m3")
    zkq = mxq(zk, 0, "e4m3")
    s = queryq.T @ zkq
    w = np.maximum(s, 0.0)
    wo1 = w * f64(os)
    wt1 = wo1.T
    vt1 = f64(vals)[:, idx].T
    wt1q = mxq(wt1, 0, "e4m3")
    vt1q = mxq(vt1, 0, "e4m3")
    o = wt1q.T @ vt1q
    return o

@@ -1,0 +1,154 @@
+from contextlib import ExitStack
+
+import concourse.mybir as mybir
+from concourse.masks import make_identity
+
+D, T, I, Q, E, U = 512, 2048, 512, 128, 512, 1024
+FLOPS = 2 * D * I * Q + 2 * I * Q * E
+
+F32 = mybir.dt.float32
+BF16 = mybir.dt.bfloat16
+U32 = mybir.dt.uint32
+U16 = mybir.dt.uint16
+U8 = mybir.dt.uint8
+FP8X4 = mybir.dt.float8_e4m3fn_x4
+ALU = mybir.AluOpType
+ACT = mybir.ActivationFunctionType
+
+P = 128
+PACK = 4
+LIST_COLS = I // 16
+E_BLOCKS = E // P
+
+
+def quantize(nc, pool, grouped, width, name):
+    codes = pool.tile([P, width], U32, name=name + "_codes", align_bytes=64)
+    scales = pool.tile([P, width], U8, name=name + "_scales", align_bytes=64)
+    nc.vector.quantize_mx(out=codes[:].bitcast(FP8X4), scales=scales[:], in_=grouped)
+    return codes, scales
+
+
+def tile_attend_keyapart_read_lean_kernel(tc, query, keys, notes, slot_factor, vals, offs, offs2, out):
+    nc = tc.nc
+    with ExitStack() as ctx:
+        lists = ctx.enter_context(tc.tile_pool(name="lists", bufs=1))
+        held = ctx.enter_context(tc.tile_pool(name="held", bufs=1))
+        psum = ctx.enter_context(tc.psum_pool(name="psum", bufs=1))
+
+        token_list = lists.tile([P, LIST_COLS], U16, name="token_list")
+        note_list = lists.tile([P, LIST_COLS], U16, name="note_list")
+        key_planes = [held.tile([P, T], F32, name=f"keys{j}") for j in range(PACK)]
+        note_planes = [held.tile([P, U], F32, name=f"notes{j}") for j in range(PACK)]
+        val_blocks = [held.tile([P, T], F32, name=f"vals{b}") for b in range(E_BLOCKS)]
+        query_raw = held.tile([P, PACK, Q], F32, name="query_raw")
+        factor = held.tile([P, PACK], F32, name="factor")
+
+        keys_by_plane = keys.rearrange("(p j) t -> p j t", j=PACK)
+        notes_by_plane = notes.rearrange("(p j) u -> p j u", j=PACK)
+        nc.sync.dma_start(note_planes[0][:], notes_by_plane[:, 0, :])
+        nc.sync.dma_start(note_list[:], offs2)
+        nc.sync.dma_start(token_list[:], offs)
+        nc.sync.dma_start(key_planes[0][:], keys_by_plane[:, 0, :])
+        nc.sync.dma_start(query_raw[:], query.rearrange("(p j) q -> p j q", j=PACK))
+        nc.sync.dma_start(factor[:], slot_factor.rearrange("o (p t) -> (o p) t", t=PACK))
+        for j in range(1, PACK):
+            nc.sync.dma_start(note_planes[j][:], notes_by_plane[:, j, :])
+            nc.sync.dma_start(key_planes[j][:], keys_by_plane[:, j, :])
+        for b in range(E_BLOCKS):
+            nc.sync.dma_start(val_blocks[b][:], vals[b * P : (b + 1) * P, :])
+
+        identity = held.tile([P, P], F32, name="identity")
+        make_identity(nc, identity[:])
+
+        query_grouped = held.tile([P, Q, PACK], BF16, name="query_grouped", align_bytes=64)
+        nc.vector.tensor_copy(query_grouped[:], query_raw[:].rearrange("p j q -> p q j"))
+        q_codes, q_scales = quantize(nc, held, query_grouped[:].rearrange("p q j -> p (q j)"), Q, "query")
+
+        apart_pairs = held.tile([P, 2, I, 2], BF16, name="apart_pairs")
+        for u in range(2):
+            difference = held.tile([P, 2, I], F32, name=f"difference{u}")
+            for h in range(2):
+                j = 2 * u + h
+                picked_notes = held.tile([P, I], F32, name=f"picked_notes{j}")
+                nc.scalar.activation(picked_notes[:], note_planes[j][:].indirect(note_list[:]), ACT.Copy)
+                nc.vector.tensor_tensor(
+                    difference[:, h, :], key_planes[j][:].indirect(token_list[:]), picked_notes[:], ALU.subtract
+                )
+            nc.scalar.activation(
+                apart_pairs[:, u].rearrange("p (t s) h -> p s t h", t=PACK),
+                difference[:].rearrange("p h (s t) -> p s t h", t=PACK),
+                ACT.Abs,
+            )
+        apart_grouped = held.tile([P, I * PACK], BF16, name="apart_grouped", align_bytes=64)
+        nc.vector.tensor_copy(
+            apart_grouped[:].bitcast(F32).rearrange("p (c u) -> p c u", u=2),
+            apart_pairs[:].rearrange("p u c h -> p u (c h)").bitcast(F32).rearrange("p u c -> p c u"),
+        )
+        z_codes, z_scales = quantize(nc, held, apart_grouped[:], I, "apart")
+
+        scores = psum.tile([P, PACK, Q], F32, name="scores")
+        for t in range(PACK):
+            cols = slice(t * P, (t + 1) * P)
+            nc.tensor.matmul_mx(
+                out=scores[:, t, :],
+                lhsT=z_codes[:, cols].bitcast(FP8X4),
+                lhsT_scale=z_scales[:, cols],
+                rhs=q_codes[:].bitcast(FP8X4),
+                rhs_scale=q_scales[:],
+                start=True,
+                stop=True,
+            )
+        weights_grouped = held.tile([P, Q, PACK], BF16, name="weights_grouped", align_bytes=64)
+        nc.vector.scalar_tensor_tensor(
+            weights_grouped[:],
+            scores[:].rearrange("p t q -> p q t"),
+            0.0,
+            factor[:].unsqueeze(1).to_broadcast([P, Q, PACK]),
+            ALU.max,
+            ALU.mult,
+        )
+        w_codes, w_scales = quantize(nc, held, weights_grouped[:].rearrange("p q t -> p (q t)"), Q, "weights")
+
+        last = E_BLOCKS - 1
+        half = I // 2
+        v_codes = held.tile([P, E], U32, name="vals_codes", align_bytes=64)
+        v_scales = held.tile([P, E], U8, name="vals_scales", align_bytes=64)
+
+        def turn_and_quantize(b, bank):
+            picked = held.tile([P, I], BF16, name=f"picked_vals{b}")
+            nc.vector.tensor_copy(picked[:, :half], val_blocks[b][:].indirect(token_list[:, : LIST_COLS // 2]))
+            nc.scalar.activation(
+                picked[:, half:], val_blocks[b][:].indirect(token_list[:, LIST_COLS // 2 :]), ACT.Copy
+            )
+            words = picked[:].bitcast(F32)
+            turned = psum.tile([P, 2, P], F32, name=f"turned{b}", tag=bank)
+            for u in range(2):
+                nc.tensor.transpose(turned[:, u, :], words[:, u : half : 2], identity[:])
+            vals_grouped = held.tile([P, P * PACK], BF16, name=f"vals_grouped{b}", align_bytes=64)
+            grouped_words = vals_grouped[:].bitcast(F32).rearrange("p (e u) -> p e u", u=2)
+            nc.scalar.copy(grouped_words, turned[:].rearrange("p u e -> p e u"))
+            cols = slice(b * P, (b + 1) * P)
+            nc.vector.quantize_mx(out=v_codes[:, cols].bitcast(FP8X4), scales=v_scales[:, cols], in_=vals_grouped[:])
+
+        def multiply(cols, bank):
+            sums = psum.tile([P, cols.stop - cols.start], F32, name=f"sums{cols.start}", tag=bank)
+            nc.tensor.matmul_mx(
+                out=sums[:],
+                lhsT=w_codes[:].bitcast(FP8X4),
+                lhsT_scale=w_scales[:],
+                rhs=v_codes[:, cols].bitcast(FP8X4),
+                rhs_scale=v_scales[:, cols],
+                start=True,
+                stop=True,
+            )
+            return sums
+
+        for b in range(E_BLOCKS):
+            turn_and_quantize(b, f"bank{b}")
+        early_out = held.tile([P, 2 * P], F32, name="early_out")
+        late_out = held.tile([P, 2 * P], F32, name="late_out")
+        nc.scalar.copy(early_out[:], multiply(slice(0, 2 * P), "bank0")[:])
+        nc.sync.dma_start(out[:, : 2 * P], early_out[:])
+        nc.scalar.copy(late_out[:, :P], multiply(slice(2 * P, 3 * P), "bank3")[:])
+        nc.vector.tensor_copy(late_out[:, P:], multiply(slice(3 * P, 4 * P), "bank2")[:])
+        nc.sync.dma_start(out[:, 2 * P :], late_out[:])

@@ -38,21 +38,19 @@ def tile_attend_keyapart_read_lean_kernel(tc, query, keys, notes, slot_factor, v
         token_list = lists.tile([P, LIST_COLS], U16, name="token_list")
         note_list = lists.tile([P, LIST_COLS], U16, name="note_list")
         key_planes = [held.tile([P, T], F32, name=f"keys{j}") for j in range(PACK)]
-        note_planes = [held.tile([P, U], F32, name=f"notes{j}") for j in range(PACK)]
-        val_blocks = [held.tile([P, T], F32, name=f"vals{b}") for b in range(E_BLOCKS)]
+        note_planes = held.tile([P, PACK * U], F32, name="notes")
+        val_blocks = [held.tile([P, T], F32, name=f"vals{b}", tag=f"vals{b}", align_bytes=64) for b in range(E_BLOCKS)]
         query_raw = held.tile([P, PACK, Q], F32, name="query_raw")
         factor = held.tile([P, PACK], F32, name="factor")
 
         keys_by_plane = keys.rearrange("(p j) t -> p j t", j=PACK)
-        notes_by_plane = notes.rearrange("(p j) u -> p j u", j=PACK)
-        nc.sync.dma_start(note_planes[0][:], notes_by_plane[:, 0, :])
+        nc.sync.dma_start(note_planes[:], notes.rearrange("(p j) u -> p (j u)", j=PACK))
         nc.sync.dma_start(note_list[:], offs2)
         nc.sync.dma_start(token_list[:], offs)
         nc.sync.dma_start(key_planes[0][:], keys_by_plane[:, 0, :])
         nc.sync.dma_start(query_raw[:], query.rearrange("(p j) q -> p j q", j=PACK))
         nc.sync.dma_start(factor[:], slot_factor.rearrange("o (p t) -> (o p) t", t=PACK))
         for j in range(1, PACK):
-            nc.sync.dma_start(note_planes[j][:], notes_by_plane[:, j, :])
             nc.sync.dma_start(key_planes[j][:], keys_by_plane[:, j, :])
         for b in range(E_BLOCKS):
             nc.sync.dma_start(val_blocks[b][:], vals[b * P : (b + 1) * P, :])
@@ -67,18 +65,25 @@ def tile_attend_keyapart_read_lean_kernel(tc, query, keys, notes, slot_factor, v
         apart_pairs = held.tile([P, 2, I, 2], BF16, name="apart_pairs")
         for u in range(2):
             difference = held.tile([P, 2, I], F32, name=f"difference{u}")
+            pieces = 1 + u
             for h in range(2):
                 j = 2 * u + h
                 picked_notes = held.tile([P, I], F32, name=f"picked_notes{j}")
-                nc.scalar.activation(picked_notes[:], note_planes[j][:].indirect(note_list[:]), ACT.Copy)
-                nc.vector.tensor_tensor(
-                    difference[:, h, :], key_planes[j][:].indirect(token_list[:]), picked_notes[:], ALU.subtract
+                nc.vector.tensor_copy(picked_notes[:], note_planes[:, j * U : (j + 1) * U].indirect(note_list[:]))
+                cuts = pieces if h == 1 else 1
+                for c in range(cuts):
+                    slots = slice(c * I // cuts, (c + 1) * I // cuts)
+                    entries = token_list[:, c * LIST_COLS // cuts : (c + 1) * LIST_COLS // cuts]
+                    nc.vector.tensor_tensor(
+                        difference[:, h, slots], key_planes[j][:].indirect(entries), picked_notes[:, slots], ALU.subtract
+                    )
+            for c in range(pieces):
+                rows = slice(c * P // pieces, (c + 1) * P // pieces)
+                nc.scalar.activation(
+                    apart_pairs[:, u].rearrange("p (t s) h -> p s t h", t=PACK)[:, rows],
+                    difference[:].rearrange("p h (s t) -> p s t h", t=PACK)[:, rows],
+                    ACT.Abs,
                 )
-            nc.scalar.activation(
-                apart_pairs[:, u].rearrange("p (t s) h -> p s t h", t=PACK),
-                difference[:].rearrange("p h (s t) -> p s t h", t=PACK),
-                ACT.Abs,
-            )
         apart_grouped = held.tile([P, I * PACK], BF16, name="apart_grouped", align_bytes=64)
         nc.vector.tensor_copy(
             apart_grouped[:].bitcast(F32).rearrange("p (c u) -> p c u", u=2),
@@ -114,24 +119,28 @@ def tile_attend_keyapart_read_lean_kernel(tc, query, keys, notes, slot_factor, v
         v_codes = held.tile([P, E], U32, name="vals_codes", align_bytes=64)
         v_scales = held.tile([P, E], U8, name="vals_scales", align_bytes=64)
 
-        def turn_and_quantize(b, bank):
+        def gather_and_turn(b):
             picked = held.tile([P, I], BF16, name=f"picked_vals{b}")
-            nc.vector.tensor_copy(picked[:, :half], val_blocks[b][:].indirect(token_list[:, : LIST_COLS // 2]))
-            nc.scalar.activation(
-                picked[:, half:], val_blocks[b][:].indirect(token_list[:, LIST_COLS // 2 :]), ACT.Copy
-            )
+            if b < 2:
+                nc.scalar.activation(picked[:], val_blocks[b][:].indirect(token_list[:]), ACT.Copy)
+            else:
+                nc.vector.tensor_copy(picked[:, :half], val_blocks[b][:].indirect(token_list[:, : LIST_COLS // 2]))
+                nc.scalar.activation(
+                    picked[:, half:], val_blocks[b][:].indirect(token_list[:, LIST_COLS // 2 :]), ACT.Copy
+                )
             words = picked[:].bitcast(F32)
-            turned = psum.tile([P, 2, P], F32, name=f"turned{b}", tag=bank)
+            turned = psum.tile([P, 2, P], F32, name=f"turned{b}")
             for u in range(2):
                 nc.tensor.transpose(turned[:, u, :], words[:, u : half : 2], identity[:])
-            vals_grouped = held.tile([P, P * PACK], BF16, name=f"vals_grouped{b}", align_bytes=64)
-            grouped_words = vals_grouped[:].bitcast(F32).rearrange("p (e u) -> p e u", u=2)
-            nc.scalar.copy(grouped_words, turned[:].rearrange("p u e -> p e u"))
-            cols = slice(b * P, (b + 1) * P)
-            nc.vector.quantize_mx(out=v_codes[:, cols].bitcast(FP8X4), scales=v_scales[:, cols], in_=vals_grouped[:])
+            return turned
 
-        def multiply(cols, bank):
-            sums = psum.tile([P, cols.stop - cols.start], F32, name=f"sums{cols.start}", tag=bank)
+        def group_and_quantize(b, turned, words):
+            nc.scalar.copy(words.rearrange("p (e u) -> p e u", u=2), turned[:].rearrange("p u e -> p e u"))
+            cols = slice(b * P, (b + 1) * P)
+            nc.vector.quantize_mx(out=v_codes[:, cols].bitcast(FP8X4), scales=v_scales[:, cols], in_=words.bitcast(BF16))
+
+        def multiply(cols):
+            sums = psum.tile([P, cols.stop - cols.start], F32, name=f"sums{cols.start}")
             nc.tensor.matmul_mx(
                 out=sums[:],
                 lhsT=w_codes[:].bitcast(FP8X4),
@@ -143,12 +152,17 @@ def tile_attend_keyapart_read_lean_kernel(tc, query, keys, notes, slot_factor, v
             )
             return sums
 
+        turned = [gather_and_turn(b) for b in range(E_BLOCKS)]
         for b in range(E_BLOCKS):
-            turn_and_quantize(b, f"bank{b}")
-        early_out = held.tile([P, 2 * P], F32, name="early_out")
-        late_out = held.tile([P, 2 * P], F32, name="late_out")
-        nc.scalar.copy(early_out[:], multiply(slice(0, 2 * P), "bank0")[:])
-        nc.sync.dma_start(out[:, : 2 * P], early_out[:])
-        nc.scalar.copy(late_out[:, :P], multiply(slice(2 * P, 3 * P), "bank3")[:])
-        nc.vector.tensor_copy(late_out[:, P:], multiply(slice(3 * P, 4 * P), "bank2")[:])
-        nc.sync.dma_start(out[:, 2 * P :], late_out[:])
+            reused = held.tile([P, 4 * P], F32, name=f"after_vals{b + 1}", tag=f"vals{b + 1}", align_bytes=64)
+            group_and_quantize(b, turned[b], reused[:, : 2 * P])
+            if b == 2:
+                early_out = reused[:, 2 * P :]
+        nc.vector.tensor_copy(early_out, multiply(slice(0, 2 * P))[:])
+        nc.sync.dma_start(out[:, : 2 * P], early_out)
+        third_out = held.tile([P, P], F32, name="third_out")
+        nc.scalar.copy(third_out[:], multiply(slice(2 * P, 3 * P))[:])
+        nc.sync.dma_start(out[:, 2 * P : 3 * P], third_out[:])
+        last_out = held.tile([P, P], F32, name="last_out")
+        nc.vector.tensor_copy(last_out[:], multiply(slice(3 * P, 4 * P))[:])
+        nc.sync.dma_start(out[:, 3 * P :], last_out[:])

@@ -48,8 +48,8 @@ def tile_attend_keyapart_read_lean_kernel(tc, query, keys, notes, slot_factor, v
         nc.sync.dma_start(note_list[:], offs2)
         nc.sync.dma_start(token_list[:], offs)
         nc.sync.dma_start(key_planes[0][:], keys_by_plane[:, 0, :])
-        nc.sync.dma_start(query_raw[:], query.rearrange("(p j) q -> p j q", j=PACK))
-        nc.sync.dma_start(factor[:], slot_factor.rearrange("o (p t) -> (o p) t", t=PACK))
+        nc.scalar.dma_start(query_raw[:], query.rearrange("(p j) q -> p j q", j=PACK))
+        nc.scalar.dma_start(factor[:], slot_factor.rearrange("o (p t) -> (o p) t", t=PACK))
         for j in range(1, PACK):
             nc.sync.dma_start(key_planes[j][:], keys_by_plane[:, j, :])
         for b in range(E_BLOCKS):
@@ -70,7 +70,12 @@ def tile_attend_keyapart_read_lean_kernel(tc, query, keys, notes, slot_factor, v
                 j = 2 * u + h
                 picked_notes = held.tile([P, I], F32, name=f"picked_notes{j}")
                 nc.vector.tensor_copy(picked_notes[:], note_planes[:, j * U : (j + 1) * U].indirect(note_list[:]))
-                cuts = pieces if h == 1 else 1
+                if u == 0:
+                    picked_keys = held.tile([P, I], F32, name=f"picked_keys{j}")
+                    nc.scalar.activation(picked_keys[:], key_planes[j][:].indirect(token_list[:]), ACT.Copy)
+                    nc.vector.tensor_tensor(difference[:, h, :], picked_keys[:], picked_notes[:], ALU.subtract)
+                    continue
+                cuts = 1 + h
                 for c in range(cuts):
                     slots = slice(c * I // cuts, (c + 1) * I // cuts)
                     entries = token_list[:, c * LIST_COLS // cuts : (c + 1) * LIST_COLS // cuts]

from contextlib import ExitStack

import concourse.mybir as mybir
from concourse.masks import make_identity

D, T, I, Q, E, U = 512, 2048, 512, 128, 512, 1024
FLOPS = 2 * D * I * Q + 2 * I * Q * E

F32 = mybir.dt.float32
BF16 = mybir.dt.bfloat16
U32 = mybir.dt.uint32
U16 = mybir.dt.uint16
U8 = mybir.dt.uint8
FP8X4 = mybir.dt.float8_e4m3fn_x4
ALU = mybir.AluOpType
ACT = mybir.ActivationFunctionType

P = 128
PACK = 4
LIST_COLS = I // 16
E_BLOCKS = E // P


def quantize(nc, pool, grouped, width, name):
    codes = pool.tile([P, width], U32, name=name + "_codes", align_bytes=64)
    scales = pool.tile([P, width], U8, name=name + "_scales", align_bytes=64)
    nc.vector.quantize_mx(out=codes[:].bitcast(FP8X4), scales=scales[:], in_=grouped)
    return codes, scales


def tile_attend_keyapart_read_lean_kernel(tc, query, keys, notes, slot_factor, vals, offs, offs2, out):
    nc = tc.nc
    with ExitStack() as ctx:
        lists = ctx.enter_context(tc.tile_pool(name="lists", bufs=1))
        held = ctx.enter_context(tc.tile_pool(name="held", bufs=1))
        psum = ctx.enter_context(tc.psum_pool(name="psum", bufs=1))

        token_list = lists.tile([P, LIST_COLS], U16, name="token_list")
        note_list = lists.tile([P, LIST_COLS], U16, name="note_list")
        key_planes = [held.tile([P, T], F32, name=f"keys{j}") for j in range(PACK)]
        note_planes = held.tile([P, PACK * U], F32, name="notes")
        val_blocks = [held.tile([P, T], F32, name=f"vals{b}", tag=f"vals{b}", align_bytes=64) for b in range(E_BLOCKS)]
        query_raw = held.tile([P, PACK, Q], F32, name="query_raw")
        factor = held.tile([P, PACK], F32, name="factor")

        keys_by_plane = keys.rearrange("(p j) t -> p j t", j=PACK)
        nc.sync.dma_start(note_planes[:], notes.rearrange("(p j) u -> p (j u)", j=PACK))
        nc.sync.dma_start(note_list[:], offs2)
        nc.sync.dma_start(token_list[:], offs)
        nc.sync.dma_start(key_planes[0][:], keys_by_plane[:, 0, :])
        nc.scalar.dma_start(query_raw[:], query.rearrange("(p j) q -> p j q", j=PACK))
        nc.scalar.dma_start(factor[:], slot_factor.rearrange("o (p t) -> (o p) t", t=PACK))
        for j in range(1, PACK):
            nc.sync.dma_start(key_planes[j][:], keys_by_plane[:, j, :])
        for b in range(E_BLOCKS):
            nc.sync.dma_start(val_blocks[b][:], vals[b * P : (b + 1) * P, :])

        identity = held.tile([P, P], F32, name="identity")
        make_identity(nc, identity[:])

        query_grouped = held.tile([P, Q, PACK], BF16, name="query_grouped", align_bytes=64)
        nc.vector.tensor_copy(query_grouped[:], query_raw[:].rearrange("p j q -> p q j"))
        q_codes, q_scales = quantize(nc, held, query_grouped[:].rearrange("p q j -> p (q j)"), Q, "query")

        apart_pairs = held.tile([P, 2, I, 2], BF16, name="apart_pairs")
        for u in range(2):
            difference = held.tile([P, 2, I], F32, name=f"difference{u}")
            pieces = 1 + u
            for h in range(2):
                j = 2 * u + h
                picked_notes = held.tile([P, I], F32, name=f"picked_notes{j}")
                nc.vector.tensor_copy(picked_notes[:], note_planes[:, j * U : (j + 1) * U].indirect(note_list[:]))
                if u == 0:
                    picked_keys = held.tile([P, I], F32, name=f"picked_keys{j}")
                    nc.scalar.activation(picked_keys[:], key_planes[j][:].indirect(token_list[:]), ACT.Copy)
                    nc.vector.tensor_tensor(difference[:, h, :], picked_keys[:], picked_notes[:], ALU.subtract)
                    continue
                cuts = 1 + h
                for c in range(cuts):
                    slots = slice(c * I // cuts, (c + 1) * I // cuts)
                    entries = token_list[:, c * LIST_COLS // cuts : (c + 1) * LIST_COLS // cuts]
                    nc.vector.tensor_tensor(
                        difference[:, h, slots], key_planes[j][:].indirect(entries), picked_notes[:, slots], ALU.subtract
                    )
            for c in range(pieces):
                rows = slice(c * P // pieces, (c + 1) * P // pieces)
                nc.scalar.activation(
                    apart_pairs[:, u].rearrange("p (t s) h -> p s t h", t=PACK)[:, rows],
                    difference[:].rearrange("p h (s t) -> p s t h", t=PACK)[:, rows],
                    ACT.Abs,
                )
        apart_grouped = held.tile([P, I * PACK], BF16, name="apart_grouped", align_bytes=64)
        nc.vector.tensor_copy(
            apart_grouped[:].bitcast(F32).rearrange("p (c u) -> p c u", u=2),
            apart_pairs[:].rearrange("p u c h -> p u (c h)").bitcast(F32).rearrange("p u c -> p c u"),
        )
        z_codes, z_scales = quantize(nc, held, apart_grouped[:], I, "apart")

        scores = psum.tile([P, PACK, Q], F32, name="scores")
        for t in range(PACK):
            cols = slice(t * P, (t + 1) * P)
            nc.tensor.matmul_mx(
                out=scores[:, t, :],
                lhsT=z_codes[:, cols].bitcast(FP8X4),
                lhsT_scale=z_scales[:, cols],
                rhs=q_codes[:].bitcast(FP8X4),
                rhs_scale=q_scales[:],
                start=True,
                stop=True,
            )
        weights_grouped = held.tile([P, Q, PACK], BF16, name="weights_grouped", align_bytes=64)
        nc.vector.scalar_tensor_tensor(
            weights_grouped[:],
            scores[:].rearrange("p t q -> p q t"),
            0.0,
            factor[:].unsqueeze(1).to_broadcast([P, Q, PACK]),
            ALU.max,
            ALU.mult,
        )
        w_codes, w_scales = quantize(nc, held, weights_grouped[:].rearrange("p q t -> p (q t)"), Q, "weights")

        last = E_BLOCKS - 1
        half = I // 2
        v_codes = held.tile([P, E], U32, name="vals_codes", align_bytes=64)
        v_scales = held.tile([P, E], U8, name="vals_scales", align_bytes=64)

        def gather_and_turn(b):
            picked = held.tile([P, I], BF16, name=f"picked_vals{b}")
            if b < 2:
                nc.scalar.activation(picked[:], val_blocks[b][:].indirect(token_list[:]), ACT.Copy)
            else:
                nc.vector.tensor_copy(picked[:, :half], val_blocks[b][:].indirect(token_list[:, : LIST_COLS // 2]))
                nc.scalar.activation(
                    picked[:, half:], val_blocks[b][:].indirect(token_list[:, LIST_COLS // 2 :]), ACT.Copy
                )
            words = picked[:].bitcast(F32)
            turned = psum.tile([P, 2, P], F32, name=f"turned{b}")
            for u in range(2):
                nc.tensor.transpose(turned[:, u, :], words[:, u : half : 2], identity[:])
            return turned

        def group_and_quantize(b, turned, words):
            nc.scalar.copy(words.rearrange("p (e u) -> p e u", u=2), turned[:].rearrange("p u e -> p e u"))
            cols = slice(b * P, (b + 1) * P)
            nc.vector.quantize_mx(out=v_codes[:, cols].bitcast(FP8X4), scales=v_scales[:, cols], in_=words.bitcast(BF16))

        def multiply(cols):
            sums = psum.tile([P, cols.stop - cols.start], F32, name=f"sums{cols.start}")
            nc.tensor.matmul_mx(
                out=sums[:],
                lhsT=w_codes[:].bitcast(FP8X4),
                lhsT_scale=w_scales[:],
                rhs=v_codes[:, cols].bitcast(FP8X4),
                rhs_scale=v_scales[:, cols],
                start=True,
                stop=True,
            )
            return sums

        turned = [gather_and_turn(b) for b in range(E_BLOCKS)]
        for b in range(E_BLOCKS):
            reused = held.tile([P, 4 * P], F32, name=f"after_vals{b + 1}", tag=f"vals{b + 1}", align_bytes=64)
            group_and_quantize(b, turned[b], reused[:, : 2 * P])
            if b == 2:
                early_out = reused[:, 2 * P :]
        nc.vector.tensor_copy(early_out, multiply(slice(0, 2 * P))[:])
        nc.sync.dma_start(out[:, : 2 * P], early_out)
        third_out = held.tile([P, P], F32, name="third_out")
        nc.scalar.copy(third_out[:], multiply(slice(2 * P, 3 * P))[:])
        nc.sync.dma_start(out[:, 2 * P : 3 * P], third_out[:])
        last_out = held.tile([P, P], F32, name="last_out")
        nc.vector.tensor_copy(last_out[:], multiply(slice(3 * P, 4 * P))[:])
        nc.sync.dma_start(out[:, 3 * P :], last_out[:])
